import numpy as np
import ml_dtypes


def mxq(x, axis, fmt="e4m3"):
    dtype, down = {"e4m3": (ml_dtypes.float8_e4m3fn, 7), "e5m2": (ml_dtypes.float8_e5m2, 14)}[fmt]
    v = np.moveaxis(np.asarray(x, np.float32).astype(ml_dtypes.bfloat16).astype(np.float64), axis, -1)
    blocks = v.reshape(v.shape[:-1] + (-1, 32))
    amax = np.abs(blocks).max(-1, keepdims=True)
    byte = np.maximum(np.where(amax > 0, np.frexp(amax)[1] - 1 + 127, 0) - down, 1)
    scale = np.exp2(byte - 127.0)
    codes = (blocks / scale).astype(np.float32).astype(dtype).astype(np.float64)
    return np.moveaxis((codes * scale).reshape(v.shape), -1, axis)


WIDE = False


def mx_kscale(k):
    if not WIDE:
        return np.ones(k)
    levels = np.array([10, -10, 5, -5, 0])
    if k % 512:
        return np.exp2(np.random.permutation(np.resize(levels, k // 32))).repeat(32)
    a = np.empty((k // 512, 16))
    for p in range(k // 512):
        a[p, :8] = np.random.permutation(np.resize(levels, 8))
        for g in range(8):
            far = levels[np.abs(levels - a[p, g]) >= 10]
            a[p, g + 8] = far[np.random.randint(len(far))]
    return np.exp2(a.ravel()).repeat(32)


BF16 = ml_dtypes.bfloat16


def bf(x):
    return np.asarray(x, np.float32).astype(BF16)


def f64(x):
    return np.asarray(x).astype(np.float64)


E2M1 = np.array([0.0, 0.5, 1.0, 1.5, 2.0, 3.0, 4.0, 6.0, -0.0, -0.5, -1.0, -1.5, -2.0, -3.0, -4.0, -6.0])


def pack_weight(w, fmt):
    k, n = w.shape
    w = f64(bf(w)).reshape(k // 32, 32, n)
    amax = np.abs(w).max(1)
    if fmt == "e4m3":
        byte = np.frexp(amax)[1] - 1 + 127 - 7
    else:
        mant, ex = np.frexp(amax / 6.0)
        byte = np.where(mant > 0.5, ex, ex - 1) + 127
    byte = np.clip(np.where(amax > 0, byte, 1), 1, 254)
    scaled = (w * np.exp2(127.0 - byte)[:, None, :]).reshape(k, n).astype(np.float32)
    by_word = np.ascontiguousarray(scaled.reshape(k // 512, 128, 4, n).transpose(0, 1, 3, 2))
    if fmt == "e4m3":
        words = by_word.astype(ml_dtypes.float8_e4m3fn).view(np.uint8)
    else:
        c = by_word.astype(ml_dtypes.float4_e2m1fn).view(np.uint8) & 0xF
        words = c[..., 0::2] | (c[..., 1::2] << 4)
    return np.ascontiguousarray(words), np.ascontiguousarray(byte.astype(np.uint8).reshape(k // 512, 16, n))


def unpack_weight(words, scales, fmt):
    g, p, n, _ = words.shape
    if fmt == "e4m3":
        vals = np.ascontiguousarray(words).view(ml_dtypes.float8_e4m3fn).astype(np.float64)
    else:
        nib = np.empty((g, p, n, 4), np.uint8)
        nib[..., 0::2] = words & 0xF
        nib[..., 1::2] = words >> 4
        vals = E2M1[nib]
    vals = vals * np.repeat(np.exp2(scales.astype(np.float64) - 127.0), 8, axis=1)[..., None]
    return vals.transpose(0, 1, 3, 2).reshape(g * 512, n)

E4M3FN = np.array([(-1.0 if i & 128 else 1.0) * ((1.0 + (i & 7) / 8.0) * 2.0 ** (((i >> 3) & 15) - 7) if i & 120 else (i & 7) * 2.0 ** -9) for i in range(256)])


def e4m3fn_bytes(y):
    return np.clip(np.asarray(y, np.float64), -448.0, 448.0).astype(np.float32).astype(ml_dtypes.float8_e4m3fn).view(np.uint8)


def e4m3fn_values(b):
    return E4M3FN[b]


S, R, H, D, Q, L = 4096, 512, 2, 512, 1024, 8
P = H * D
F = D // 2
C = S // L


def rotate_interleaved(x, theta):
    cos = np.cos(theta)[:, None, :]
    sin = np.sin(theta)[:, None, :]
    even = x[..., 0::2]
    odd = x[..., 1::2]
    new_even = even * cos - odd * sin
    new_odd = even * sin + odd * cos
    return np.stack([new_even, new_odd], axis=-1).reshape(x.shape)


def chunk_means(k):
    s, h, d = k.shape
    return np.mean(k.reshape(s // L, L, h, d), axis=1)


def logsumexp(v):
    m = np.max(v, axis=-1, keepdims=True)
    return m + np.log(np.sum(np.exp(v - m), axis=-1, keepdims=True))


def draw0():
    r, t = mx_kscale(R), mx_kscale(P)
    a = bf(np.random.standard_normal((S, R)) * r)
    b_words, b_scales = pack_weight(np.random.standard_normal((R, P)) / np.sqrt(R) / r[:, None] * t, "e4m3")
    return {
        "a": a,
        "b_words": b_words,
        "b_scales": b_scales,
        "theta": bf(np.random.uniform(-3.14, 3.14, (S, F))),
        "q": bf(np.random.standard_normal((H, Q, D)) * 1.06 * np.sqrt(L) / t.reshape(H, 1, D)),
    }


def core(a, b_words, b_scales, theta, q):
    a, theta, q = f64(a), f64(theta), f64(q)
    s = a.shape[0]
    h, _, d = q.shape
    k0 = (mxq(a, 1, "e4m3") @ unpack_weight(b_words, b_scales, "e4m3")).reshape(s, h, d)
    k = rotate_interleaved(k0, theta)
    lm = chunk_means(k)
    sc = (mxq(q, 2, "e4m3") @ mxq(lm, 2, "e4m3").transpose(1, 2, 0)) / np.sqrt(d)
    c = lm.shape[0]
    return sc - logsumexp(sc) + np.log(c)


def setup_inputs():
    drawn = draw0()
    full = np.asarray(drawn['a']).astype(np.float64)
    scale = (np.abs(full).reshape(32, 128, 4, 128).max(axis=(1, 3)) / 448.0).astype(np.float32)
    given = {}
    for key, value in drawn.items():
        if key == 'a':
            given['a_bytes'] = e4m3fn_bytes(full / np.repeat(np.repeat(scale.astype(np.float64), 128, axis=0), 128, axis=1))
            given['a_scale'] = scale
        else:
            given[key] = value
    return given


def reference(a_bytes, a_scale, b_words, b_scales, theta, q):
    return core(e4m3fn_values(a_bytes) * np.repeat(np.repeat(a_scale.astype(np.float64), 128, axis=0), 128, axis=1), b_words, b_scales, theta, q)

@@ -1,0 +1,541 @@
+import math
+from contextlib import ExitStack
+
+import concourse.mybir as mybir
+from concourse.masks import make_identity
+
+F32 = mybir.dt.float32
+BF16 = mybir.dt.bfloat16
+U32 = mybir.dt.uint32
+I32 = mybir.dt.int32
+U8 = mybir.dt.uint8
+FP8 = mybir.dt.float8_e4m3fn
+FP8X4 = mybir.dt.float8_e4m3fn_x4
+ALU = mybir.AluOpType
+ACT = mybir.ActivationFunctionType
+AX = mybir.AxisListType
+
+S, R, H, D, Q, L = 4096, 512, 2, 512, 1024, 8
+C = S // L
+P = 128
+NG = 4
+FLOPS = 2 * S * R * H * D + 2 * H * Q * D * C
+ALPHA = 1.0 / math.sqrt(D)
+HALF_PI = math.pi / 2
+WIDEN_V = 3
+
+
+def tile_lowrankpreropekeylandmarkscores_d2p_kernel(tc, a_bytes, a_scale, b_words, b_scales, theta, q, out):
+    nc = tc.nc
+    V, A, G, T, SY = nc.vector, nc.scalar, nc.gpsimd, nc.tensor, nc.sync
+    with ExitStack() as ctx:
+        keep = ctx.enter_context(tc.tile_pool(name="keep", bufs=1))
+        work = ctx.enter_context(tc.tile_pool(name="work", bufs=2))
+        psum = ctx.enter_context(tc.psum_pool(name="psum", bufs=1))
+        ctx.enter_context(tc.manual_schedule())
+
+        araw, thraw, qraw = {}, {}, {}
+
+        def load_a(g, ap):
+            t = work.tile([P, 2, R], U8, name="a_raw", bufs=8, align_bytes=64)
+            src = a_bytes[1024 * g : 1024 * (g + 1), :].rearrange("(c t) k -> c t k", t=8)
+            SY.dma_start(out=t[:], in_=src[:, 2 * ap : 2 * ap + 2, :])
+            araw[g, ap] = t
+
+        def load_theta(g, hh):
+            t = work.tile([P, 4, 256], BF16, name="th_raw", bufs=4, align_bytes=64)
+            src = theta[1024 * g : 1024 * (g + 1), :].rearrange("(c t) j -> c t j", t=8)
+            SY.dma_start(out=t[:], in_=src[:, 4 * hh : 4 * hh + 4, :])
+            thraw[g, hh] = t
+
+        def load_q(h, qh):
+            t = work.tile([P, 4, D], BF16, name="q_raw", bufs=2, align_bytes=64)
+            src = q[h].rearrange("(p i) d -> p i d", i=8)
+            SY.dma_start(out=t[:], in_=src[:, 4 * qh : 4 * qh + 4, :])
+            qraw[h, qh] = t
+
+        load_a(0, 0)
+        asc = keep.tile([P, NG, 4], F32, name="asc")
+        asc_src = a_scale.rearrange("(g i) j -> i g j", i=8)
+        for i in range(8):
+            A.dma_start(out=asc[16 * i : 16 * i + 16, :, :], in_=asc_src[i].partition_broadcast(16))
+        bw = keep.tile([P, H * D], U32, name="bw", align_bytes=64)
+        bs = keep.tile([P, H * D], U8, name="bs", align_bytes=64)
+        V.memset(bs[:].bitcast(I32), 0)
+        for qd in range(4):
+            A.dma_start(out=bs[32 * qd : 32 * qd + 4, :].bitcast(I32), in_=b_scales[0, 4 * qd : 4 * qd + 4, :].bitcast(I32))
+        load_theta(0, 0)
+        bw_src = b_words[0].rearrange("p n t -> p (n t)")
+        SY.dma_start(out=bw[:, 0:512].bitcast(I32), in_=bw_src[:, 0:2048].bitcast(I32))
+        load_a(0, 1)
+        load_a(0, 2)
+        load_theta(0, 1)
+        load_a(0, 3)
+        SY.dma_start(out=bw[:, 512:1024].bitcast(I32), in_=bw_src[:, 2048:4096].bitcast(I32))
+
+        ident = keep.tile([P, P], F32, name="ident")
+        make_identity(nc, ident[:])
+
+        qq, qqs, lmq, lmqs, sc, mx1, mx2 = [], [], [], [], [], [], []
+        nm12, s12 = [], []
+        for h in range(H):
+            qq.append(keep.tile([P, 1024], U32, name="qq%d" % h, align_bytes=64))
+            qqs.append(keep.tile([P, 1024], U8, name="qqs%d" % h, align_bytes=64))
+            lmq.append(keep.tile([P, C], U32, name="lmq%d" % h, align_bytes=64))
+            lmqs.append(keep.tile([P, C], U8, name="lmqs%d" % h, align_bytes=64))
+            sc.append(keep.tile([P, 8, C], F32, name="sc%d" % h))
+            mx1.append(keep.tile([P, 8], F32, name="mxa%d" % h))
+            mx2.append(keep.tile([P, 8], F32, name="mxb%d" % h))
+            nm12.append(keep.tile([P, 8], F32, name="nm%d" % h))
+            s12.append(keep.tile([P, 8], F32, name="s12%d" % h))
+
+        aw, at, aq, aqs = {}, {}, {}, {}
+
+        def widen(g, ap, parts, on_v):
+            if (g, ap) not in aw:
+                aw[g, ap] = work.tile([P, 2, R], BF16, name="aw", bufs=3, align_bytes=64)
+            for x in parts:
+                i, j = divmod(x, 4)
+                dst = aw[g, ap][:, i, 128 * j : 128 * j + 128]
+                src = araw[g, ap][:, i, 128 * j : 128 * j + 128].bitcast(FP8)
+                s_ap = asc[:, g, j : j + 1]
+                if x in on_v:
+                    V.tensor_scalar(out=dst, in0=src, scalar1=s_ap, scalar2=None, op0=ALU.mult)
+                else:
+                    A.activation(out=dst, in_=src, func=ACT.Copy, scale=s_ap)
+
+        def a_transpose(g, ap):
+            words = aw[g, ap][:].rearrange("p t k -> p (t k)").bitcast(F32)
+            xt = psum.tile([P, 2, 2, P], F32, name="misc", bufs=1)
+            for i in range(2):
+                for u in range(2):
+                    T.transpose(xt[:, i, u, :], words[:, 256 * i + u : 256 * i + 256 : 2], ident[:])
+            return xt
+
+        def a_evac(g, ap, xt, eng):
+            t = work.tile([P, 1024], BF16, name="at", bufs=5, align_bytes=64)
+            at[g, ap] = t
+            dst = t[:].bitcast(F32).rearrange("p (i c u) -> p i c u", i=2, u=2)
+            src = xt[:].rearrange("p i u c -> p i c u")
+            if eng == "v":
+                V.tensor_copy(out=dst, in_=src)
+            else:
+                A.copy(out=dst, in_=src)
+
+        def a_quant(g, ap):
+            if g not in aq:
+                aq[g] = work.tile([P, 1024], U32, name="aq", bufs=2, align_bytes=64)
+                aqs[g] = work.tile([P, 1024], U8, name="aqs", bufs=2, align_bytes=64)
+            cols = slice(256 * ap, 256 * ap + 256)
+            V.quantize_mx(out=aq[g][:, cols].bitcast(FP8X4), scales=aqs[g][:, cols], in_=at[g, ap][:])
+
+        ath, ctab, stab, s2 = {}, {}, {}, {}
+
+        def absolute(g, hh):
+            t = work.tile([P, 4, 256], BF16, name="ath", bufs=3, align_bytes=64)
+            ath[g, hh] = t
+            V.tensor_single_scalar(
+                out=t[:].rearrange("p t j -> p (t j)").bitcast(I32),
+                in_=thraw[g, hh][:].rearrange("p t j -> p (t j)").bitcast(I32),
+                scalar=0x7FFF7FFF,
+                op=ALU.bitwise_and,
+            )
+
+        def table_tiles(g):
+            if g not in ctab:
+                ctab[g] = work.tile([P, 8, 2, P], F32, name="ctab", bufs=2)
+                stab[g] = work.tile([P, 8, 2, P], F32, name="stab", bufs=2)
+                s2[g] = work.tile([P, 2, 2, 2, P], F32, name="s2", bufs=2)
+
+        def table_cos(g, tp):
+            table_tiles(g)
+            x = 2 * tp - 4 * (tp // 2)
+            src = ath[g, tp // 2][:, x : x + 2, :].rearrange("p t (j u) -> p t u j", u=2)
+            A.activation(out=ctab[g][:, 2 * tp : 2 * tp + 2, :, :], in_=src, func=ACT.Sin, scale=-1.0, bias=HALF_PI)
+
+        def table_sin(g, tp):
+            table_tiles(g)
+            x = 2 * tp - 4 * (tp // 2)
+            src = thraw[g, tp // 2][:, x : x + 2, :].rearrange("p t (j u) -> p t u j", u=2)
+            A.activation(out=stab[g][:, 2 * tp : 2 * tp + 2, :, :], in_=src, func=ACT.Sin)
+
+        def table_s2(g):
+            table_tiles(g)
+            src = thraw[g, 0][:, 0:2, :].rearrange("p t (j u) -> p t u j", u=2)
+            A.activation(out=s2[g][:, :, :, 0, :], in_=src, func=ACT.Sin)
+            A.activation(out=s2[g][:, :, :, 1, :], in_=src, func=ACT.Sin, scale=-1.0)
+
+        k0, prod = {}, {}
+
+        def mx(s):
+            g, h, k = s // 8, (s // 4) % 2, s % 4
+            for i in range(2):
+                t = 2 * k + i
+                bank = psum.tile([P, D], F32, name="k0", bufs=3)
+                T.matmul_mx(
+                    out=bank[:],
+                    lhsT=aq[g][:, P * t : P * t + P].bitcast(FP8X4),
+                    lhsT_scale=aqs[g][:, P * t : P * t + P],
+                    rhs=bw[:, D * h : D * h + D].bitcast(FP8X4),
+                    rhs_scale=bs[:, D * h : D * h + D],
+                    start=True,
+                    stop=True,
+                )
+                k0[s, i] = bank
+
+        def is_g(s):
+            return s >= 4 and s % 4 == 0
+
+        def new_prod(s):
+            if is_g(s):
+                prod[s] = work.tile([P, 2, 2, 2, 2, P], F32, name="prodg", bufs=2)
+            else:
+                prod[s] = work.tile([P, 2, 2, 2, 2, P], F32, name="prodv", bufs=3)
+
+        def k0_view(s, i):
+            return k0[s, i][:].rearrange("s (p u e) -> s u e p", u=2, e=2)
+
+        def products_v(s, i):
+            g, k = s // 8, s % 4
+            t = 2 * k + i
+            if i == 0:
+                new_prod(s)
+            x = k0_view(s, i)
+            pr = prod[s]
+            cb = ctab[g][:, t, :, :].unsqueeze(2).broadcast_to([P, 2, 2, P])
+            V.tensor_tensor(out=pr[:, 0, i, :, :, :], in0=x, in1=cb, op=ALU.mult)
+            V.tensor_tensor(out=pr[:, 1, i, :, 0, :], in0=x[:, :, 0, :], in1=stab[g][:, t, :, :], op=ALU.mult)
+            V.scalar_tensor_tensor(
+                out=pr[:, 1, i, :, 1, :], in0=x[:, :, 1, :], scalar=-1.0, in1=stab[g][:, t, :, :], op0=ALU.mult, op1=ALU.mult
+            )
+
+        def products_g(s):
+            g, k = s // 8, s % 4
+            new_prod(s)
+            kc = work.tile([P, 2, 2, 2, P], F32, name="kc", bufs=2)
+            for i in range(2):
+                A.copy(out=kc[:, i, :, :, :], in_=k0_view(s, i))
+            pr = prod[s]
+            cb = ctab[g][:, 0:2, :, :].rearrange("p t u j -> p (t u) j").unsqueeze(2).broadcast_to([P, 4, 2, P])
+            G.tensor_tensor(
+                out=pr[:, 0, :, :, :, :].rearrange("p t u e j -> p (t u) e j"),
+                in0=kc[:].rearrange("p t u e j -> p (t u) e j"),
+                in1=cb,
+                op=ALU.mult,
+            )
+            G.tensor_tensor(
+                out=pr[:, 1, :, :, :, :].rearrange("p t u e j -> p (t u e j)"),
+                in0=kc[:].rearrange("p t u e j -> p (t u e j)"),
+                in1=s2[g][:].rearrange("p t u e j -> p (t u e j)"),
+                op=ALU.mult,
+            )
+
+        acc = {}
+
+        def turn_and_add(s, first, last):
+            u = s // 4
+            if first:
+                for x in range(4):
+                    acc[u, x] = psum.tile([P, P], F32, name="acc%d" % x, bufs=1)
+            for x in range(4):
+                uu, e = divmod(x, 2)
+                for i in range(2):
+                    for w in range(2):
+                        T.matmul(
+                            acc[u, x][:],
+                            lhsT=prod[s][:, w, i, uu, (e if w == 0 else 1 - e), :],
+                            rhs=ident[:],
+                            start=(first and i == 0 and w == 0),
+                            stop=(last and i == 1 and w == 1),
+                            is_transpose=True,
+                        )
+
+        lmi = {}
+
+        lmf = {}
+
+        def lm_evac(u, eng):
+            f = work.tile([P, 4, P], BF16, name="lmf", bufs=2, align_bytes=64)
+            for x in range(4):
+                if eng == "v":
+                    V.tensor_scalar(out=f[:, x, :], in0=acc[u, x][:], scalar1=1.0 / L, scalar2=None, op0=ALU.mult)
+                else:
+                    A.activation(out=f[:, x, :], in_=acc[u, x][:], func=ACT.Copy, scale=1.0 / L)
+            lmf[u] = f
+
+        def lm_mix(u):
+            t = work.tile([P, P, 4], BF16, name="lmi", bufs=2, align_bytes=64)
+            V.tensor_copy(out=t[:], in_=lmf[u][:].rearrange("p x c -> p c x"))
+            lmi[u] = t
+
+        def lm_quant(u):
+            g, h = u // 2, u % 2
+            cols = slice(P * g, P * g + P)
+            V.quantize_mx(
+                out=lmq[h][:, cols].bitcast(FP8X4), scales=lmqs[h][:, cols], in_=lmi[u][:].rearrange("p c x -> p (c x)")
+            )
+
+        qt = {}
+
+        def q_transpose(h, qp):
+            words = qraw[h, qp // 2][:].rearrange("p i d -> p (i d)").bitcast(F32)
+            xt = psum.tile([P, 2, 2, P], F32, name="misc", bufs=1)
+            for i in range(2):
+                o = 256 * (2 * (qp % 2) + i)
+                for u in range(2):
+                    T.transpose(xt[:, i, u, :], words[:, o + u : o + 256 : 2], ident[:])
+            return xt
+
+        def q_evac(h, qp, xt):
+            t = work.tile([P, 1024], BF16, name="qt", bufs=5, align_bytes=64)
+            qt[h, qp] = t
+            A.copy(out=t[:].bitcast(F32).rearrange("p (i c u) -> p i c u", i=2, u=2), in_=xt[:].rearrange("p i u c -> p i c u"))
+
+        def q_quant(h, qp):
+            cols = slice(256 * qp, 256 * qp + 256)
+            V.quantize_mx(out=qq[h][:, cols].bitcast(FP8X4), scales=qqs[h][:, cols], in_=qt[h, qp][:])
+
+        def scores(h, tiles, c0, n, tag):
+            if tag == "misc":
+                bank = psum.tile([P, len(tiles), n], F32, name="misc", bufs=1)
+            else:
+                bank = psum.tile([P, len(tiles), n], F32, name="k0", bufs=3)
+            for x, i in enumerate(tiles):
+                T.matmul_mx(
+                    out=bank[:, x, :],
+                    lhsT=qq[h][:, P * i : P * i + P].bitcast(FP8X4),
+                    lhsT_scale=qqs[h][:, P * i : P * i + P],
+                    rhs=lmq[h][:, c0 : c0 + n].bitcast(FP8X4),
+                    rhs_scale=lmqs[h][:, c0 : c0 + n],
+                    start=True,
+                    stop=True,
+                )
+            return bank
+
+        def scores_evac(h, tiles, c0, n, bank, mxt):
+            for x, i in enumerate(tiles):
+                V.tensor_scalar(
+                    out=sc[h][:, i, c0 : c0 + n],
+                    in0=bank[:, x, :],
+                    scalar1=ALPHA,
+                    scalar2=None,
+                    op0=ALU.mult,
+                    op1=ALU.max,
+                    accum_out=mxt[:, i : i + 1],
+                )
+
+        def max12(h):
+            m = work.tile([P, 8], F32, name="m12", bufs=2)
+            V.tensor_tensor(out=m[:], in0=mx1[h][:], in1=mx2[h][:], op=ALU.max)
+            V.tensor_scalar(out=nm12[h][:], in0=m[:], scalar1=-1.0, scalar2=None, op0=ALU.mult)
+
+        def exp12(h, i):
+            junk = work.tile([P, 384], BF16, name="junk", bufs=2)
+            A.activation(
+                out=junk[:], in_=sc[h][:, i, 0:384], func=ACT.Exp, bias=nm12[h][:, i : i + 1], accum_out=s12[h][:, i : i + 1]
+            )
+
+        mx3, nm3, d3, s3, ln3, bias3 = {}, {}, {}, {}, {}, {}
+
+        def last_max(h, x, bank):
+            if h not in mx3:
+                mx3[h] = keep.tile([P, 8], F32, name="mx3%d" % h)
+            V.tensor_reduce(out=mx3[h][:, 4 * x : 4 * x + 4], in_=bank[:], axis=AX.X, op=ALU.max)
+            A.activation(out=sc[h][:, 4 * x : 4 * x + 4, 384:512], in_=bank[:], func=ACT.Copy, scale=ALPHA)
+
+        def last_shift(h):
+            nm3[h] = keep.tile([P, 8], F32, name="nmf%d" % h)
+            d3[h] = keep.tile([P, 8], F32, name="dd%d" % h)
+            V.scalar_tensor_tensor(out=nm3[h][:], in0=mx3[h][:], scalar=-ALPHA, in1=nm12[h][:], op0=ALU.mult, op1=ALU.min)
+            V.tensor_tensor(out=d3[h][:], in0=nm3[h][:], in1=nm12[h][:], op=ALU.subtract)
+
+        def last_exps(h):
+            s3[h] = keep.tile([P, 9, 8], F32, name="s3%d" % h)
+            for i in range(8):
+                junk = work.tile([P, 384], BF16, name="junk", bufs=2)
+                A.activation(
+                    out=junk[:, 0:128],
+                    in_=sc[h][:, i, 384:512],
+                    func=ACT.Exp,
+                    bias=nm3[h][:, i : i + 1],
+                    accum_out=s3[h][:, 0, i : i + 1],
+                )
+            A.activation(out=s3[h][:, 1, :], in_=d3[h][:], func=ACT.Exp)
+
+        def last_log(h):
+            tot = keep.tile([P, 8], F32, name="tot%d" % h)
+            V.tensor_tensor(out=tot[:], in0=s12[h][:], in1=s3[h][:, 1, :], op=ALU.mult)
+            V.tensor_tensor(out=tot[:], in0=tot[:], in1=s3[h][:, 0, :], op=ALU.add)
+            ln3[h] = keep.tile([P, 8], F32, name="ln%d" % h)
+            A.activation(out=ln3[h][:], in_=tot[:], func=ACT.Ln, scale=1.0 / C)
+
+        def last_bias(h):
+            bias3[h] = keep.tile([P, 8], F32, name="bias%d" % h)
+            V.tensor_tensor(out=bias3[h][:], in0=nm3[h][:], in1=ln3[h][:], op=ALU.subtract)
+
+        def last_out(h, engines):
+            dst = out[h].rearrange("(p i) c -> p i c", i=8)
+            for i in range(8):
+                row = sc[h][:, i, :]
+                b = bias3[h][:, i : i + 1]
+                if engines[i] == "a":
+                    A.activation(out=row, in_=row, func=ACT.Identity, bias=b)
+                elif engines[i] == "g":
+                    G.tensor_scalar(out=row, in0=row, scalar1=1.0, scalar2=b, op0=ALU.mult, op1=ALU.add)
+                else:
+                    V.tensor_scalar(out=row, in0=row, scalar1=b, scalar2=None, op0=ALU.add)
+                if i % 2 == 1:
+                    SY.dma_start(out=dst[:, i - 1 : i + 1, :], in_=sc[h][:, i - 1 : i + 1, :])
+
+        V_HEAD = (0, 1, 2, 3, 4)
+        absolute(0, 0)
+        widen(0, 0, range(8), V_HEAD)
+        xt = a_transpose(0, 0)
+        table_cos(0, 0)
+        table_sin(0, 0)
+        a_evac(0, 0, xt, "v")
+        a_quant(0, 0)
+        mx(0)
+        widen(0, 1, range(8), V_HEAD)
+        xt = a_transpose(0, 1)
+        a_evac(0, 1, xt, "v")
+        a_quant(0, 1)
+        products_v(0, 0)
+        products_v(0, 1)
+        table_cos(0, 1)
+        table_sin(0, 1)
+        absolute(0, 1)
+        load_theta(1, 0)
+
+        on_v = tuple(range(WIDEN_V))
+        q_beats = {}
+        for x in range(4):
+            q_beats[6 + x] = (0, x)
+            q_beats[14 + x] = (1, x)
+        q_quants = {9: 0, 17: 1}
+        score_beats = {}
+        for x in range(4):
+            score_beats[15 + x] = (0, (2 * x, 2 * x + 1), 0, 256, mx1[0])
+            score_beats[19 + x] = (1, (2 * x, 2 * x + 1), 0, 256, mx1[1])
+        for x in range(2):
+            score_beats[23 + x] = (0, tuple(range(4 * x, 4 * x + 4)), 256, 128, mx2[0])
+            score_beats[27 + x] = (1, tuple(range(4 * x, 4 * x + 4)), 256, 128, mx2[1])
+        soft = {
+            0: [lambda g: table_s2(g)],
+            1: [lambda g: table_cos(g, 0)],
+            2: [lambda g: table_cos(g, 1)],
+            3: [lambda g: table_sin(g, 1)],
+            4: [lambda g: table_cos(g, 2)],
+            5: [lambda g: table_sin(g, 2)],
+            6: [lambda g: table_cos(g, 3)],
+            7: [lambda g: table_sin(g, 3)],
+        }
+
+        for b in range(32):
+            g, r, u, k = b // 8, b % 8, b // 4, b % 4
+            if r == 0 and g + 1 < NG:
+                for ap in range(4):
+                    load_a(g + 1, ap)
+                    if ap == 2:
+                        load_theta(g + 1, ap // 2)
+                if g == 0:
+                    load_q(0, 0)
+                    load_q(0, 1)
+            if r == 5 and g + 2 < NG:
+                load_theta(g + 2, 0)
+            if b in (9, 10):
+                load_q(1, b - 9)
+            if b + 1 < 32:
+                mx(b + 1)
+            sbank = None
+            if b in score_beats:
+                h_s, tiles, c0, n, mxt = score_beats[b]
+                sbank = scores(h_s, tiles, c0, n, "k0")
+            if b == 31:
+                for x in range(2):
+                    last_max(0, x, scores(0, tuple(range(4 * x, 4 * x + 4)), 384, 128, "k0"))
+            if k == 1 and u > 0:
+                lm_evac(u - 1, "a")
+            if g == 0 and b < 2:
+                widen(0, b + 2, range(8), (0, 1, 2))
+                xt = a_transpose(0, b + 2)
+                a_evac(0, b + 2, xt, "v")
+                a_quant(0, b + 2)
+                table_cos(0, b + 2)
+                table_sin(0, b + 2)
+            if g + 1 < NG:
+                if g == 0 and r == 0:
+                    table_s2(0)
+                for f in soft[r]:
+                    f(g + 1)
+                ap = r - 1
+                if 0 <= ap < 4:
+                    widen(g + 1, ap, [x for x in range(8) if x not in on_v], on_v)
+            if 26 <= b < 30:
+                exp12(0, 2 * (b - 26))
+                exp12(0, 2 * (b - 26) + 1)
+            if 30 <= b < 32:
+                for x in range(4):
+                    exp12(1, 4 * (b - 30) + x)
+            if k < 3:
+                products_v(b + 1, 0)
+                products_v(b + 1, 1)
+            elif b + 1 < 32:
+                products_g(b + 1)
+            if sbank is not None:
+                scores_evac(h_s, tiles, c0, n, sbank, mxt)
+            if b == 0:
+                absolute(1, 0)
+            if g + 1 < NG and 2 <= r <= 5:
+                xt = a_transpose(g + 1, r - 2)
+                a_evac(g + 1, r - 2, xt, "a")
+            if b in q_beats:
+                xt = q_transpose(*q_beats[b])
+                q_evac(*q_beats[b], xt)
+            if u == 0:
+                if k < 3:
+                    turn_and_add(k, k == 0, False)
+            else:
+                if k == 0:
+                    turn_and_add(4 * u - 1, False, True)
+                elif k < 3:
+                    turn_and_add(4 * u + k, k == 1, False)
+                else:
+                    turn_and_add(4 * u, False, False)
+            if k == 1:
+                if u > 0:
+                    lm_mix(u - 1)
+                if r == 1 and g + 1 < NG:
+                    absolute(g + 1, 1)
+                    for ap in range(4):
+                        widen(g + 1, ap, on_v, on_v)
+                if r == 5 and g + 2 < NG:
+                    absolute(g + 2, 0)
+                if r == 5 and g + 1 < NG:
+                    for ap in range(4):
+                        a_quant(g + 1, ap)
+                if b in q_quants:
+                    for qp in range(4):
+                        q_quant(q_quants[b], qp)
+                if u > 0:
+                    lm_quant(u - 1)
+                if b == 25:
+                    max12(0)
+                if b == 29:
+                    max12(1)
+        turn_and_add(31, False, True)
+        last_shift(0)
+        last_exps(0)
+        last_log(0)
+        last_bias(0)
+        lm_evac(7, "v")
+        lm_mix(7)
+        lm_quant(7)
+        last_out(0, "gagagaga")
+        for x in range(2):
+            last_max(1, x, scores(1, tuple(range(4 * x, 4 * x + 4)), 384, 128, "k0"))
+        last_shift(1)
+        last_exps(1)
+        last_log(1)
+        last_bias(1)
+        last_out(1, "avgvavgv")

@@ -22,7 +22,9 @@ NG = 4
 FLOPS = 2 * S * R * H * D + 2 * H * Q * D * C
 ALPHA = 1.0 / math.sqrt(D)
 HALF_PI = math.pi / 2
-WIDEN_V = 3
+PSUM_BUFS = {"k0": 3, "misc": 1}
+G_PAIRS = (4, 8, 12, 16, 18, 20, 22, 24, 26, 28)
+MIX_A = (0, 1, 2, 3, 4, 5, 6)
 
 
 def tile_lowrankpreropekeylandmarkscores_d2p_kernel(tc, a_bytes, a_scale, b_words, b_scales, theta, q, out):
@@ -54,17 +56,18 @@ def tile_lowrankpreropekeylandmarkscores_d2p_kernel(tc, a_bytes, a_scale, b_word
             SY.dma_start(out=t[:], in_=src[:, 4 * qh : 4 * qh + 4, :])
             qraw[h, qh] = t
 
-        load_a(0, 0)
         asc = keep.tile([P, NG, 4], F32, name="asc")
         asc_src = a_scale.rearrange("(g i) j -> i g j", i=8)
         for i in range(8):
-            A.dma_start(out=asc[16 * i : 16 * i + 16, :, :], in_=asc_src[i].partition_broadcast(16))
+            eng = SY if i % 2 == 0 else A
+            eng.dma_start(out=asc[16 * i : 16 * i + 16, :, :], in_=asc_src[i].partition_broadcast(16))
+        load_a(0, 0)
+        load_theta(0, 0)
         bw = keep.tile([P, H * D], U32, name="bw", align_bytes=64)
         bs = keep.tile([P, H * D], U8, name="bs", align_bytes=64)
         V.memset(bs[:].bitcast(I32), 0)
         for qd in range(4):
             A.dma_start(out=bs[32 * qd : 32 * qd + 4, :].bitcast(I32), in_=b_scales[0, 4 * qd : 4 * qd + 4, :].bitcast(I32))
-        load_theta(0, 0)
         bw_src = b_words[0].rearrange("p n t -> p (n t)")
         SY.dma_start(out=bw[:, 0:512].bitcast(I32), in_=bw_src[:, 0:2048].bitcast(I32))
         load_a(0, 1)
@@ -93,7 +96,7 @@ def tile_lowrankpreropekeylandmarkscores_d2p_kernel(tc, a_bytes, a_scale, b_word
 
         def widen(g, ap, parts, on_v):
             if (g, ap) not in aw:
-                aw[g, ap] = work.tile([P, 2, R], BF16, name="aw", bufs=3, align_bytes=64)
+                aw[g, ap] = work.tile([P, 2, R], BF16, name="aw", bufs=4, align_bytes=64)
             for x in parts:
                 i, j = divmod(x, 4)
                 dst = aw[g, ap][:, i, 128 * j : 128 * j + 128]
@@ -104,9 +107,9 @@ def tile_lowrankpreropekeylandmarkscores_d2p_kernel(tc, a_bytes, a_scale, b_word
                 else:
                     A.activation(out=dst, in_=src, func=ACT.Copy, scale=s_ap)
 
-        def a_transpose(g, ap):
+        def a_transpose(g, ap, tag="misc"):
             words = aw[g, ap][:].rearrange("p t k -> p (t k)").bitcast(F32)
-            xt = psum.tile([P, 2, 2, P], F32, name="misc", bufs=1)
+            xt = psum.tile([P, 2, 2, P], F32, name=tag, bufs=PSUM_BUFS[tag])
             for i in range(2):
                 for u in range(2):
                     T.transpose(xt[:, i, u, :], words[:, 256 * i + u : 256 * i + 256 : 2], ident[:])
@@ -141,29 +144,40 @@ def tile_lowrankpreropekeylandmarkscores_d2p_kernel(tc, a_bytes, a_scale, b_word
                 op=ALU.bitwise_and,
             )
 
+        def on_g(s):
+            return s in G_PAIRS
+
         def table_tiles(g):
             if g not in ctab:
                 ctab[g] = work.tile([P, 8, 2, P], F32, name="ctab", bufs=2)
                 stab[g] = work.tile([P, 8, 2, P], F32, name="stab", bufs=2)
                 s2[g] = work.tile([P, 2, 2, 2, P], F32, name="s2", bufs=2)
 
-        def table_cos(g, tp):
-            table_tiles(g)
-            x = 2 * tp - 4 * (tp // 2)
-            src = ath[g, tp // 2][:, x : x + 2, :].rearrange("p t (j u) -> p t u j", u=2)
-            A.activation(out=ctab[g][:, 2 * tp : 2 * tp + 2, :, :], in_=src, func=ACT.Sin, scale=-1.0, bias=HALF_PI)
+        def angles(src, g, t0, n):
+            return src[g, t0 // 4][:, t0 % 4 : t0 % 4 + n, :].rearrange("p t (j u) -> p t u j", u=2)
 
-        def table_sin(g, tp):
+        def table_cos(g, t0, n):
             table_tiles(g)
-            x = 2 * tp - 4 * (tp // 2)
-            src = thraw[g, tp // 2][:, x : x + 2, :].rearrange("p t (j u) -> p t u j", u=2)
-            A.activation(out=stab[g][:, 2 * tp : 2 * tp + 2, :, :], in_=src, func=ACT.Sin)
+            A.activation(
+                out=ctab[g][:, t0 : t0 + n, :, :], in_=angles(ath, g, t0, n), func=ACT.Sin, scale=-1.0, bias=HALF_PI
+            )
 
-        def table_s2(g):
+        def table_sin(g, t0, n):
             table_tiles(g)
-            src = thraw[g, 0][:, 0:2, :].rearrange("p t (j u) -> p t u j", u=2)
-            A.activation(out=s2[g][:, :, :, 0, :], in_=src, func=ACT.Sin)
-            A.activation(out=s2[g][:, :, :, 1, :], in_=src, func=ACT.Sin, scale=-1.0)
+            A.activation(out=stab[g][:, t0 : t0 + n, :, :], in_=angles(thraw, g, t0, n), func=ACT.Sin)
+
+        def table_odd(g, t0):
+            pairs = (8 * g + t0 // 2, 8 * g + 4 + t0 // 2)
+            if any(not on_g(s) for s in pairs):
+                table_sin(g, t0, 1)
+            if any(on_g(s) for s in pairs):
+                table_s2(g, t0)
+
+        def table_s2(g, t0):
+            table_tiles(g)
+            src = thraw[g, t0 // 4][:, t0 % 4, :].rearrange("p (j u) -> p u j", u=2)
+            A.activation(out=s2[g][:, t0 // 4, :, 0, :], in_=src, func=ACT.Sin)
+            A.activation(out=s2[g][:, t0 // 4, :, 1, :], in_=src, func=ACT.Sin, scale=-1.0)
 
         k0, prod = {}, {}
 
@@ -183,14 +197,8 @@ def tile_lowrankpreropekeylandmarkscores_d2p_kernel(tc, a_bytes, a_scale, b_word
                 )
                 k0[s, i] = bank
 
-        def is_g(s):
-            return s >= 4 and s % 4 == 0
-
         def new_prod(s):
-            if is_g(s):
-                prod[s] = work.tile([P, 2, 2, 2, 2, P], F32, name="prodg", bufs=2)
-            else:
-                prod[s] = work.tile([P, 2, 2, 2, 2, P], F32, name="prodv", bufs=3)
+            prod[s] = work.tile([P, 2, 2, 2, 2, P], F32, name="prod", bufs=4)
 
         def k0_view(s, i):
             return k0[s, i][:].rearrange("s (p u e) -> s u e p", u=2, e=2)
@@ -198,8 +206,6 @@ def tile_lowrankpreropekeylandmarkscores_d2p_kernel(tc, a_bytes, a_scale, b_word
         def products_v(s, i):
             g, k = s // 8, s % 4
             t = 2 * k + i
-            if i == 0:
-                new_prod(s)
             x = k0_view(s, i)
             pr = prod[s]
             cb = ctab[g][:, t, :, :].unsqueeze(2).broadcast_to([P, 2, 2, P])
@@ -211,22 +217,16 @@ def tile_lowrankpreropekeylandmarkscores_d2p_kernel(tc, a_bytes, a_scale, b_word
 
         def products_g(s):
             g, k = s // 8, s % 4
-            new_prod(s)
-            kc = work.tile([P, 2, 2, 2, P], F32, name="kc", bufs=2)
-            for i in range(2):
-                A.copy(out=kc[:, i, :, :, :], in_=k0_view(s, i))
+            t = 2 * k + 1
+            kc = work.tile([P, 2, 2, P], F32, name="kc", bufs=2)
+            A.copy(out=kc[:], in_=k0_view(s, 1))
             pr = prod[s]
-            cb = ctab[g][:, 0:2, :, :].rearrange("p t u j -> p (t u) j").unsqueeze(2).broadcast_to([P, 4, 2, P])
+            cb = ctab[g][:, t, :, :].unsqueeze(2).broadcast_to([P, 2, 2, P])
+            G.tensor_tensor(out=pr[:, 0, 1, :, :, :], in0=kc[:], in1=cb, op=ALU.mult)
             G.tensor_tensor(
-                out=pr[:, 0, :, :, :, :].rearrange("p t u e j -> p (t u) e j"),
-                in0=kc[:].rearrange("p t u e j -> p (t u) e j"),
-                in1=cb,
-                op=ALU.mult,
-            )
-            G.tensor_tensor(
-                out=pr[:, 1, :, :, :, :].rearrange("p t u e j -> p (t u e j)"),
-                in0=kc[:].rearrange("p t u e j -> p (t u e j)"),
-                in1=s2[g][:].rearrange("p t u e j -> p (t u e j)"),
+                out=pr[:, 1, 1, :, :, :].rearrange("p u e j -> p (u e j)"),
+                in0=kc[:].rearrange("p u e j -> p (u e j)"),
+                in1=s2[g][:, t // 4, :, :, :].rearrange("p u e j -> p (u e j)"),
                 op=ALU.mult,
             )
 
@@ -254,10 +254,10 @@ def tile_lowrankpreropekeylandmarkscores_d2p_kernel(tc, a_bytes, a_scale, b_word
 
         lmf = {}
 
-        def lm_evac(u, eng):
+        def lm_evac(u, engines):
             f = work.tile([P, 4, P], BF16, name="lmf", bufs=2, align_bytes=64)
             for x in range(4):
-                if eng == "v":
+                if engines[x] == "v":
                     V.tensor_scalar(out=f[:, x, :], in0=acc[u, x][:], scalar1=1.0 / L, scalar2=None, op0=ALU.mult)
                 else:
                     A.activation(out=f[:, x, :], in_=acc[u, x][:], func=ACT.Copy, scale=1.0 / L)
@@ -265,7 +265,10 @@ def tile_lowrankpreropekeylandmarkscores_d2p_kernel(tc, a_bytes, a_scale, b_word
 
         def lm_mix(u):
             t = work.tile([P, P, 4], BF16, name="lmi", bufs=2, align_bytes=64)
-            V.tensor_copy(out=t[:], in_=lmf[u][:].rearrange("p x c -> p c x"))
+            if u in MIX_A:
+                A.copy(out=t[:], in_=lmf[u][:].rearrange("p x c -> p c x"))
+            else:
+                V.tensor_copy(out=t[:], in_=lmf[u][:].rearrange("p x c -> p c x"))
             lmi[u] = t
 
         def lm_quant(u):
@@ -296,10 +299,7 @@ def tile_lowrankpreropekeylandmarkscores_d2p_kernel(tc, a_bytes, a_scale, b_word
             V.quantize_mx(out=qq[h][:, cols].bitcast(FP8X4), scales=qqs[h][:, cols], in_=qt[h, qp][:])
 
         def scores(h, tiles, c0, n, tag):
-            if tag == "misc":
-                bank = psum.tile([P, len(tiles), n], F32, name="misc", bufs=1)
-            else:
-                bank = psum.tile([P, len(tiles), n], F32, name="k0", bufs=3)
+            bank = psum.tile([P, len(tiles), n], F32, name=tag, bufs=PSUM_BUFS[tag])
             for x, i in enumerate(tiles):
                 T.matmul_mx(
                     out=bank[:, x, :],
@@ -318,16 +318,14 @@ def tile_lowrankpreropekeylandmarkscores_d2p_kernel(tc, a_bytes, a_scale, b_word
                     out=sc[h][:, i, c0 : c0 + n],
                     in0=bank[:, x, :],
                     scalar1=ALPHA,
-                    scalar2=None,
+                    scalar2=None if c0 == 0 else mx1[h][:, i : i + 1],
                     op0=ALU.mult,
                     op1=ALU.max,
                     accum_out=mxt[:, i : i + 1],
                 )
 
         def max12(h):
-            m = work.tile([P, 8], F32, name="m12", bufs=2)
-            V.tensor_tensor(out=m[:], in0=mx1[h][:], in1=mx2[h][:], op=ALU.max)
-            V.tensor_scalar(out=nm12[h][:], in0=m[:], scalar1=-1.0, scalar2=None, op0=ALU.mult)
+            A.activation(out=nm12[h][:], in_=mx2[h][:], func=ACT.Copy, scale=-1.0)
 
         def exp12(h, i):
             junk = work.tile([P, 384], BF16, name="junk", bufs=2)
@@ -362,12 +360,16 @@ def tile_lowrankpreropekeylandmarkscores_d2p_kernel(tc, a_bytes, a_scale, b_word
                 )
             A.activation(out=s3[h][:, 1, :], in_=d3[h][:], func=ACT.Exp)
 
+        tot = {}
+
+        def last_total(h):
+            tot[h] = keep.tile([P, 8], F32, name="tot%d" % h)
+            V.tensor_tensor(out=tot[h][:], in0=s12[h][:], in1=s3[h][:, 1, :], op=ALU.mult)
+            V.tensor_tensor(out=tot[h][:], in0=tot[h][:], in1=s3[h][:, 0, :], op=ALU.add)
+
         def last_log(h):
-            tot = keep.tile([P, 8], F32, name="tot%d" % h)
-            V.tensor_tensor(out=tot[:], in0=s12[h][:], in1=s3[h][:, 1, :], op=ALU.mult)
-            V.tensor_tensor(out=tot[:], in0=tot[:], in1=s3[h][:, 0, :], op=ALU.add)
             ln3[h] = keep.tile([P, 8], F32, name="ln%d" % h)
-            A.activation(out=ln3[h][:], in_=tot[:], func=ACT.Ln, scale=1.0 / C)
+            A.activation(out=ln3[h][:], in_=tot[h][:], func=ACT.Ln, scale=1.0 / C)
 
         def last_bias(h):
             bias3[h] = keep.tile([P, 8], F32, name="bias%d" % h)
@@ -387,32 +389,33 @@ def tile_lowrankpreropekeylandmarkscores_d2p_kernel(tc, a_bytes, a_scale, b_word
                 if i % 2 == 1:
                     SY.dma_start(out=dst[:, i - 1 : i + 1, :], in_=sc[h][:, i - 1 : i + 1, :])
 
-        V_HEAD = (0, 1, 2, 3, 4)
         absolute(0, 0)
-        widen(0, 0, range(8), V_HEAD)
-        xt = a_transpose(0, 0)
-        table_cos(0, 0)
-        table_sin(0, 0)
+        table_cos(0, 0, 2)
+        table_sin(0, 0, 2)
+        widen(0, 0, range(8), range(8))
+        xt = a_transpose(0, 0, "k0")
+        widen(0, 1, range(8), (0, 1, 2, 3, 4, 5))
         a_evac(0, 0, xt, "v")
+        xt = a_transpose(0, 1, "k0")
         a_quant(0, 0)
         mx(0)
-        widen(0, 1, range(8), V_HEAD)
-        xt = a_transpose(0, 1)
-        a_evac(0, 1, xt, "v")
-        a_quant(0, 1)
+        a_evac(0, 1, xt, "a")
+        table_cos(0, 2, 2)
+        table_sin(0, 2, 2)
+        widen(0, 2, range(8), (0, 1, 2, 3, 4, 5))
+        new_prod(0)
         products_v(0, 0)
+        a_quant(0, 1)
+        xt = a_transpose(0, 2)
         products_v(0, 1)
-        table_cos(0, 1)
-        table_sin(0, 1)
+        widen(0, 3, range(8), (0, 1, 2, 3, 4, 5))
+        a_evac(0, 2, xt, "a")
         absolute(0, 1)
-        load_theta(1, 0)
 
-        on_v = tuple(range(WIDEN_V))
         q_beats = {}
         for x in range(4):
             q_beats[6 + x] = (0, x)
             q_beats[14 + x] = (1, x)
-        q_quants = {9: 0, 17: 1}
         score_beats = {}
         for x in range(4):
             score_beats[15 + x] = (0, (2 * x, 2 * x + 1), 0, 256, mx1[0])
@@ -420,122 +423,142 @@ def tile_lowrankpreropekeylandmarkscores_d2p_kernel(tc, a_bytes, a_scale, b_word
         for x in range(2):
             score_beats[23 + x] = (0, tuple(range(4 * x, 4 * x + 4)), 256, 128, mx2[0])
             score_beats[27 + x] = (1, tuple(range(4 * x, 4 * x + 4)), 256, 128, mx2[1])
-        soft = {
-            0: [lambda g: table_s2(g)],
-            1: [lambda g: table_cos(g, 0)],
-            2: [lambda g: table_cos(g, 1)],
-            3: [lambda g: table_sin(g, 1)],
-            4: [lambda g: table_cos(g, 2)],
-            5: [lambda g: table_sin(g, 2)],
-            6: [lambda g: table_cos(g, 3)],
-            7: [lambda g: table_sin(g, 3)],
-        }
 
-        for b in range(32):
+        SOFT0 = [[], [0], [1], [2], [3], [4], [5, 6], [7]]
+
+        def soft(g, r):
+            if r == 0:
+                widen(g, 0, range(8), ())
+                table_odd(g, 1)
+            if r == 1:
+                widen(g, 1, range(4), ())
+            if r == 2:
+                widen(g, 1, range(4, 8), ())
+                widen(g, 2, range(8), ())
+            if r == 3:
+                widen(g, 3, range(8), ())
+            if r == 4:
+                table_cos(g, 0, 2)
+                table_sin(g, 0, 1)
+                table_cos(g, 2, 2)
+            if r == 5:
+                table_sin(g, 2, 2)
+            if r == 6:
+                table_odd(g, 5)
+                table_cos(g, 4, 2)
+                table_sin(g, 4, 1)
+            if r == 7:
+                table_cos(g, 6, 2)
+                table_sin(g, 6, 2)
+
+        for b in range(31):
             g, r, u, k = b // 8, b % 8, b // 4, b % 4
+            n = b + 1
             if r == 0 and g + 1 < NG:
                 for ap in range(4):
                     load_a(g + 1, ap)
-                    if ap == 2:
+                    if ap % 2 == 0:
                         load_theta(g + 1, ap // 2)
-                if g == 0:
-                    load_q(0, 0)
-                    load_q(0, 1)
-            if r == 5 and g + 2 < NG:
-                load_theta(g + 2, 0)
+            if b in (1, 2):
+                load_q(0, b - 1)
             if b in (9, 10):
                 load_q(1, b - 9)
-            if b + 1 < 32:
-                mx(b + 1)
+            mx(n)
+            new_prod(n)
+            if on_g(n):
+                products_g(n)
             sbank = None
             if b in score_beats:
-                h_s, tiles, c0, n, mxt = score_beats[b]
-                sbank = scores(h_s, tiles, c0, n, "k0")
-            if b == 31:
-                for x in range(2):
-                    last_max(0, x, scores(0, tuple(range(4 * x, 4 * x + 4)), 384, 128, "k0"))
+                h_s, tiles, c0, width, mxt = score_beats[b]
+                sbank = scores(h_s, tiles, c0, width, "k0" if b < 22 else "misc")
+            if b == 30:
+                p3banks = [scores(0, tuple(range(4 * x, 4 * x + 4)), 384, 128, ("k0", "misc")[x]) for x in range(2)]
             if k == 1 and u > 0:
-                lm_evac(u - 1, "a")
-            if g == 0 and b < 2:
-                widen(0, b + 2, range(8), (0, 1, 2))
-                xt = a_transpose(0, b + 2)
-                a_evac(0, b + 2, xt, "v")
-                a_quant(0, b + 2)
-                table_cos(0, b + 2)
-                table_sin(0, b + 2)
-            if g + 1 < NG:
-                if g == 0 and r == 0:
-                    table_s2(0)
-                for f in soft[r]:
-                    f(g + 1)
-                ap = r - 1
-                if 0 <= ap < 4:
-                    widen(g + 1, ap, [x for x in range(8) if x not in on_v], on_v)
-            if 26 <= b < 30:
-                exp12(0, 2 * (b - 26))
-                exp12(0, 2 * (b - 26) + 1)
-            if 30 <= b < 32:
-                for x in range(4):
-                    exp12(1, 4 * (b - 30) + x)
-            if k < 3:
-                products_v(b + 1, 0)
-                products_v(b + 1, 1)
-            elif b + 1 < 32:
-                products_g(b + 1)
-            if sbank is not None:
-                scores_evac(h_s, tiles, c0, n, sbank, mxt)
+                lm_evac(u - 1, "aaaa")
+                if u - 1 in MIX_A:
+                    lm_mix(u - 1)
             if b == 0:
-                absolute(1, 0)
-            if g + 1 < NG and 2 <= r <= 5:
-                xt = a_transpose(g + 1, r - 2)
-                a_evac(g + 1, r - 2, xt, "a")
+                a_quant(0, 2)
+                xt = a_transpose(0, 3)
+                a_evac(0, 3, xt, "a")
+                table_cos(0, 4, 2)
+                table_sin(0, 4, 1)
+                table_odd(0, 5)
+            if b == 1:
+                a_quant(0, 3)
+                table_cos(0, 6, 2)
+                table_sin(0, 6, 2)
+                table_s2(0, 1)
+            if g + 1 < NG:
+                if g == 0:
+                    for x in SOFT0[r]:
+                        soft(1, x)
+                else:
+                    soft(g + 1, r)
+            if b == 25:
+                max12(0)
+            if b == 29:
+                max12(1)
+            if b in (25, 26, 29, 30):
+                for x in range(3 if b == 30 else 4):
+                    exp12(b // 29, 4 * ((b - 1) % 4 % 2) + x)
+            if r == 1 and g + 1 < NG:
+                absolute(g + 1, 0)
+                absolute(g + 1, 1)
+            if g + 1 < NG and r == 5:
+                a_quant(g + 1, 0)
+                if g > 0:
+                    a_quant(g + 1, 1)
+            if g + 1 < NG and r == 7:
+                if g == 0:
+                    a_quant(g + 1, 1)
+                a_quant(g + 1, 2)
+                a_quant(g + 1, 3)
+            if b in (9, 11, 17, 19):
+                for x in range(2):
+                    q_quant(b // 17, 2 * ((b % 4) // 2) + x)
+            products_v(n, 0)
+            if sbank is not None and b < 22:
+                scores_evac(h_s, tiles, c0, width, sbank, mxt)
+            if b == 29:
+                lm_quant(6)
+            if not on_g(n):
+                products_v(n, 1)
+            if sbank is not None and b >= 22:
+                scores_evac(h_s, tiles, c0, width, sbank, mxt)
+            if b == 30:
+                last_max(0, 0, p3banks[0])
+                last_max(0, 1, p3banks[1])
+                last_shift(0)
+                last_exps(0)
+            if k == 2 and 0 < u < 7:
+                if u - 1 not in MIX_A:
+                    lm_mix(u - 1)
+                lm_quant(u - 1)
+            ap = r - (3 if g == 0 else 2)
+            if g + 1 < NG and 0 <= ap < 4:
+                xt = a_transpose(g + 1, ap)
+                a_evac(g + 1, ap, xt, "a")
             if b in q_beats:
                 xt = q_transpose(*q_beats[b])
                 q_evac(*q_beats[b], xt)
-            if u == 0:
-                if k < 3:
-                    turn_and_add(k, k == 0, False)
-            else:
-                if k == 0:
-                    turn_and_add(4 * u - 1, False, True)
-                elif k < 3:
-                    turn_and_add(4 * u + k, k == 1, False)
-                else:
-                    turn_and_add(4 * u, False, False)
-            if k == 1:
-                if u > 0:
-                    lm_mix(u - 1)
-                if r == 1 and g + 1 < NG:
-                    absolute(g + 1, 1)
-                    for ap in range(4):
-                        widen(g + 1, ap, on_v, on_v)
-                if r == 5 and g + 2 < NG:
-                    absolute(g + 2, 0)
-                if r == 5 and g + 1 < NG:
-                    for ap in range(4):
-                        a_quant(g + 1, ap)
-                if b in q_quants:
-                    for qp in range(4):
-                        q_quant(q_quants[b], qp)
-                if u > 0:
-                    lm_quant(u - 1)
-                if b == 25:
-                    max12(0)
-                if b == 29:
-                    max12(1)
+            if b >= 1:
+                turn_and_add(b - 1, (b - 1) % 4 == 0, (b - 1) % 4 == 3)
+        turn_and_add(30, False, False)
         turn_and_add(31, False, True)
-        last_shift(0)
-        last_exps(0)
-        last_log(0)
-        last_bias(0)
-        lm_evac(7, "v")
+        lm_evac(7, "vvvv")
         lm_mix(7)
         lm_quant(7)
-        last_out(0, "gagagaga")
+        last_total(0)
+        last_log(0)
+        exp12(1, 7)
+        last_bias(0)
+        last_out(0, "vavvavva")
         for x in range(2):
-            last_max(1, x, scores(1, tuple(range(4 * x, 4 * x + 4)), 384, 128, "k0"))
+            last_max(1, x, scores(1, tuple(range(4 * x, 4 * x + 4)), 384, 128, ("k0", "misc")[x]))
         last_shift(1)
         last_exps(1)
+        last_total(1)
         last_log(1)
         last_bias(1)
-        last_out(1, "avgvavgv")
+        last_out(1, "vavvavva")

import math
from contextlib import ExitStack

import concourse.mybir as mybir
from concourse.masks import make_identity

F32 = mybir.dt.float32
BF16 = mybir.dt.bfloat16
U32 = mybir.dt.uint32
I32 = mybir.dt.int32
U8 = mybir.dt.uint8
FP8 = mybir.dt.float8_e4m3fn
FP8X4 = mybir.dt.float8_e4m3fn_x4
ALU = mybir.AluOpType
ACT = mybir.ActivationFunctionType
AX = mybir.AxisListType

S, R, H, D, Q, L = 4096, 512, 2, 512, 1024, 8
C = S // L
P = 128
NG = 4
FLOPS = 2 * S * R * H * D + 2 * H * Q * D * C
ALPHA = 1.0 / math.sqrt(D)
HALF_PI = math.pi / 2
PSUM_BUFS = {"k0": 3, "misc": 1}
G_PAIRS = (4, 8, 12, 16, 18, 20, 22, 24, 26, 28)
MIX_A = (0, 1, 2, 3, 4, 5, 6)


def tile_lowrankpreropekeylandmarkscores_d2p_kernel(tc, a_bytes, a_scale, b_words, b_scales, theta, q, out):
    nc = tc.nc
    V, A, G, T, SY = nc.vector, nc.scalar, nc.gpsimd, nc.tensor, nc.sync
    with ExitStack() as ctx:
        keep = ctx.enter_context(tc.tile_pool(name="keep", bufs=1))
        work = ctx.enter_context(tc.tile_pool(name="work", bufs=2))
        psum = ctx.enter_context(tc.psum_pool(name="psum", bufs=1))
        ctx.enter_context(tc.manual_schedule())

        araw, thraw, qraw = {}, {}, {}

        def load_a(g, ap):
            t = work.tile([P, 2, R], U8, name="a_raw", bufs=8, align_bytes=64)
            src = a_bytes[1024 * g : 1024 * (g + 1), :].rearrange("(c t) k -> c t k", t=8)
            SY.dma_start(out=t[:], in_=src[:, 2 * ap : 2 * ap + 2, :])
            araw[g, ap] = t

        def load_theta(g, hh):
            t = work.tile([P, 4, 256], BF16, name="th_raw", bufs=4, align_bytes=64)
            src = theta[1024 * g : 1024 * (g + 1), :].rearrange("(c t) j -> c t j", t=8)
            SY.dma_start(out=t[:], in_=src[:, 4 * hh : 4 * hh + 4, :])
            thraw[g, hh] = t

        def load_q(h, qh):
            t = work.tile([P, 4, D], BF16, name="q_raw", bufs=2, align_bytes=64)
            src = q[h].rearrange("(p i) d -> p i d", i=8)
            SY.dma_start(out=t[:], in_=src[:, 4 * qh : 4 * qh + 4, :])
            qraw[h, qh] = t

        asc = keep.tile([P, NG, 4], F32, name="asc")
        asc_src = a_scale.rearrange("(g i) j -> i g j", i=8)
        for i in range(8):
            eng = SY if i % 2 == 0 else A
            eng.dma_start(out=asc[16 * i : 16 * i + 16, :, :], in_=asc_src[i].partition_broadcast(16))
        load_a(0, 0)
        load_theta(0, 0)
        bw = keep.tile([P, H * D], U32, name="bw", align_bytes=64)
        bs = keep.tile([P, H * D], U8, name="bs", align_bytes=64)
        V.memset(bs[:].bitcast(I32), 0)
        for qd in range(4):
            A.dma_start(out=bs[32 * qd : 32 * qd + 4, :].bitcast(I32), in_=b_scales[0, 4 * qd : 4 * qd + 4, :].bitcast(I32))
        bw_src = b_words[0].rearrange("p n t -> p (n t)")
        SY.dma_start(out=bw[:, 0:512].bitcast(I32), in_=bw_src[:, 0:2048].bitcast(I32))
        load_a(0, 1)
        load_a(0, 2)
        load_theta(0, 1)
        load_a(0, 3)
        SY.dma_start(out=bw[:, 512:1024].bitcast(I32), in_=bw_src[:, 2048:4096].bitcast(I32))

        ident = keep.tile([P, P], F32, name="ident")
        make_identity(nc, ident[:])

        qq, qqs, lmq, lmqs, sc, mx1, mx2 = [], [], [], [], [], [], []
        nm12, s12 = [], []
        for h in range(H):
            qq.append(keep.tile([P, 1024], U32, name="qq%d" % h, align_bytes=64))
            qqs.append(keep.tile([P, 1024], U8, name="qqs%d" % h, align_bytes=64))
            lmq.append(keep.tile([P, C], U32, name="lmq%d" % h, align_bytes=64))
            lmqs.append(keep.tile([P, C], U8, name="lmqs%d" % h, align_bytes=64))
            sc.append(keep.tile([P, 8, C], F32, name="sc%d" % h))
            mx1.append(keep.tile([P, 8], F32, name="mxa%d" % h))
            mx2.append(keep.tile([P, 8], F32, name="mxb%d" % h))
            nm12.append(keep.tile([P, 8], F32, name="nm%d" % h))
            s12.append(keep.tile([P, 8], F32, name="s12%d" % h))

        aw, at, aq, aqs = {}, {}, {}, {}

        def widen(g, ap, parts, on_v):
            if (g, ap) not in aw:
                aw[g, ap] = work.tile([P, 2, R], BF16, name="aw", bufs=4, align_bytes=64)
            for x in parts:
                i, j = divmod(x, 4)
                dst = aw[g, ap][:, i, 128 * j : 128 * j + 128]
                src = araw[g, ap][:, i, 128 * j : 128 * j + 128].bitcast(FP8)
                s_ap = asc[:, g, j : j + 1]
                if x in on_v:
                    V.tensor_scalar(out=dst, in0=src, scalar1=s_ap, scalar2=None, op0=ALU.mult)
                else:
                    A.activation(out=dst, in_=src, func=ACT.Copy, scale=s_ap)

        def a_transpose(g, ap, tag="misc"):
            words = aw[g, ap][:].rearrange("p t k -> p (t k)").bitcast(F32)
            xt = psum.tile([P, 2, 2, P], F32, name=tag, bufs=PSUM_BUFS[tag])
            for i in range(2):
                for u in range(2):
                    T.transpose(xt[:, i, u, :], words[:, 256 * i + u : 256 * i + 256 : 2], ident[:])
            return xt

        def a_evac(g, ap, xt, eng):
            t = work.tile([P, 1024], BF16, name="at", bufs=5, align_bytes=64)
            at[g, ap] = t
            dst = t[:].bitcast(F32).rearrange("p (i c u) -> p i c u", i=2, u=2)
            src = xt[:].rearrange("p i u c -> p i c u")
            if eng == "v":
                V.tensor_copy(out=dst, in_=src)
            else:
                A.copy(out=dst, in_=src)

        def a_quant(g, ap):
            if g not in aq:
                aq[g] = work.tile([P, 1024], U32, name="aq", bufs=2, align_bytes=64)
                aqs[g] = work.tile([P, 1024], U8, name="aqs", bufs=2, align_bytes=64)
            cols = slice(256 * ap, 256 * ap + 256)
            V.quantize_mx(out=aq[g][:, cols].bitcast(FP8X4), scales=aqs[g][:, cols], in_=at[g, ap][:])

        ath, ctab, stab, s2 = {}, {}, {}, {}

        def absolute(g, hh):
            t = work.tile([P, 4, 256], BF16, name="ath", bufs=3, align_bytes=64)
            ath[g, hh] = t
            V.tensor_single_scalar(
                out=t[:].rearrange("p t j -> p (t j)").bitcast(I32),
                in_=thraw[g, hh][:].rearrange("p t j -> p (t j)").bitcast(I32),
                scalar=0x7FFF7FFF,
                op=ALU.bitwise_and,
            )

        def on_g(s):
            return s in G_PAIRS

        def table_tiles(g):
            if g not in ctab:
                ctab[g] = work.tile([P, 8, 2, P], F32, name="ctab", bufs=2)
                stab[g] = work.tile([P, 8, 2, P], F32, name="stab", bufs=2)
                s2[g] = work.tile([P, 2, 2, 2, P], F32, name="s2", bufs=2)

        def angles(src, g, t0, n):
            return src[g, t0 // 4][:, t0 % 4 : t0 % 4 + n, :].rearrange("p t (j u) -> p t u j", u=2)

        def table_cos(g, t0, n):
            table_tiles(g)
            A.activation(
                out=ctab[g][:, t0 : t0 + n, :, :], in_=angles(ath, g, t0, n), func=ACT.Sin, scale=-1.0, bias=HALF_PI
            )

        def table_sin(g, t0, n):
            table_tiles(g)
            A.activation(out=stab[g][:, t0 : t0 + n, :, :], in_=angles(thraw, g, t0, n), func=ACT.Sin)

        def table_odd(g, t0):
            pairs = (8 * g + t0 // 2, 8 * g + 4 + t0 // 2)
            if any(not on_g(s) for s in pairs):
                table_sin(g, t0, 1)
            if any(on_g(s) for s in pairs):
                table_s2(g, t0)

        def table_s2(g, t0):
            table_tiles(g)
            src = thraw[g, t0 // 4][:, t0 % 4, :].rearrange("p (j u) -> p u j", u=2)
            A.activation(out=s2[g][:, t0 // 4, :, 0, :], in_=src, func=ACT.Sin)
            A.activation(out=s2[g][:, t0 // 4, :, 1, :], in_=src, func=ACT.Sin, scale=-1.0)

        k0, prod = {}, {}

        def mx(s):
            g, h, k = s // 8, (s // 4) % 2, s % 4
            for i in range(2):
                t = 2 * k + i
                bank = psum.tile([P, D], F32, name="k0", bufs=3)
                T.matmul_mx(
                    out=bank[:],
                    lhsT=aq[g][:, P * t : P * t + P].bitcast(FP8X4),
                    lhsT_scale=aqs[g][:, P * t : P * t + P],
                    rhs=bw[:, D * h : D * h + D].bitcast(FP8X4),
                    rhs_scale=bs[:, D * h : D * h + D],
                    start=True,
                    stop=True,
                )
                k0[s, i] = bank

        def new_prod(s):
            prod[s] = work.tile([P, 2, 2, 2, 2, P], F32, name="prod", bufs=4)

        def k0_view(s, i):
            return k0[s, i][:].rearrange("s (p u e) -> s u e p", u=2, e=2)

        def products_v(s, i):
            g, k = s // 8, s % 4
            t = 2 * k + i
            x = k0_view(s, i)
            pr = prod[s]
            cb = ctab[g][:, t, :, :].unsqueeze(2).broadcast_to([P, 2, 2, P])
            V.tensor_tensor(out=pr[:, 0, i, :, :, :], in0=x, in1=cb, op=ALU.mult)
            V.tensor_tensor(out=pr[:, 1, i, :, 0, :], in0=x[:, :, 0, :], in1=stab[g][:, t, :, :], op=ALU.mult)
            V.scalar_tensor_tensor(
                out=pr[:, 1, i, :, 1, :], in0=x[:, :, 1, :], scalar=-1.0, in1=stab[g][:, t, :, :], op0=ALU.mult, op1=ALU.mult
            )

        def products_g(s):
            g, k = s // 8, s % 4
            t = 2 * k + 1
            kc = work.tile([P, 2, 2, P], F32, name="kc", bufs=2)
            A.copy(out=kc[:], in_=k0_view(s, 1))
            pr = prod[s]
            cb = ctab[g][:, t, :, :].unsqueeze(2).broadcast_to([P, 2, 2, P])
            G.tensor_tensor(out=pr[:, 0, 1, :, :, :], in0=kc[:], in1=cb, op=ALU.mult)
            G.tensor_tensor(
                out=pr[:, 1, 1, :, :, :].rearrange("p u e j -> p (u e j)"),
                in0=kc[:].rearrange("p u e j -> p (u e j)"),
                in1=s2[g][:, t // 4, :, :, :].rearrange("p u e j -> p (u e j)"),
                op=ALU.mult,
            )

        acc = {}

        def turn_and_add(s, first, last):
            u = s // 4
            if first:
                for x in range(4):
                    acc[u, x] = psum.tile([P, P], F32, name="acc%d" % x, bufs=1)
            for x in range(4):
                uu, e = divmod(x, 2)
                for i in range(2):
                    for w in range(2):
                        T.matmul(
                            acc[u, x][:],
                            lhsT=prod[s][:, w, i, uu, (e if w == 0 else 1 - e), :],
                            rhs=ident[:],
                            start=(first and i == 0 and w == 0),
                            stop=(last and i == 1 and w == 1),
                            is_transpose=True,
                        )

        lmi = {}

        lmf = {}

        def lm_evac(u, engines):
            f = work.tile([P, 4, P], BF16, name="lmf", bufs=2, align_bytes=64)
            for x in range(4):
                if engines[x] == "v":
                    V.tensor_scalar(out=f[:, x, :], in0=acc[u, x][:], scalar1=1.0 / L, scalar2=None, op0=ALU.mult)
                else:
                    A.activation(out=f[:, x, :], in_=acc[u, x][:], func=ACT.Copy, scale=1.0 / L)
            lmf[u] = f

        def lm_mix(u):
            t = work.tile([P, P, 4], BF16, name="lmi", bufs=2, align_bytes=64)
            if u in MIX_A:
                A.copy(out=t[:], in_=lmf[u][:].rearrange("p x c -> p c x"))
            else:
                V.tensor_copy(out=t[:], in_=lmf[u][:].rearrange("p x c -> p c x"))
            lmi[u] = t

        def lm_quant(u):
            g, h = u // 2, u % 2
            cols = slice(P * g, P * g + P)
            V.quantize_mx(
                out=lmq[h][:, cols].bitcast(FP8X4), scales=lmqs[h][:, cols], in_=lmi[u][:].rearrange("p c x -> p (c x)")
            )

        qt = {}

        def q_transpose(h, qp):
            words = qraw[h, qp // 2][:].rearrange("p i d -> p (i d)").bitcast(F32)
            xt = psum.tile([P, 2, 2, P], F32, name="misc", bufs=1)
            for i in range(2):
                o = 256 * (2 * (qp % 2) + i)
                for u in range(2):
                    T.transpose(xt[:, i, u, :], words[:, o + u : o + 256 : 2], ident[:])
            return xt

        def q_evac(h, qp, xt):
            t = work.tile([P, 1024], BF16, name="qt", bufs=5, align_bytes=64)
            qt[h, qp] = t
            A.copy(out=t[:].bitcast(F32).rearrange("p (i c u) -> p i c u", i=2, u=2), in_=xt[:].rearrange("p i u c -> p i c u"))

        def q_quant(h, qp):
            cols = slice(256 * qp, 256 * qp + 256)
            V.quantize_mx(out=qq[h][:, cols].bitcast(FP8X4), scales=qqs[h][:, cols], in_=qt[h, qp][:])

        def scores(h, tiles, c0, n, tag):
            bank = psum.tile([P, len(tiles), n], F32, name=tag, bufs=PSUM_BUFS[tag])
            for x, i in enumerate(tiles):
                T.matmul_mx(
                    out=bank[:, x, :],
                    lhsT=qq[h][:, P * i : P * i + P].bitcast(FP8X4),
                    lhsT_scale=qqs[h][:, P * i : P * i + P],
                    rhs=lmq[h][:, c0 : c0 + n].bitcast(FP8X4),
                    rhs_scale=lmqs[h][:, c0 : c0 + n],
                    start=True,
                    stop=True,
                )
            return bank

        def scores_evac(h, tiles, c0, n, bank, mxt):
            for x, i in enumerate(tiles):
                V.tensor_scalar(
                    out=sc[h][:, i, c0 : c0 + n],
                    in0=bank[:, x, :],
                    scalar1=ALPHA,
                    scalar2=None if c0 == 0 else mx1[h][:, i : i + 1],
                    op0=ALU.mult,
                    op1=ALU.max,
                    accum_out=mxt[:, i : i + 1],
                )

        def max12(h):
            A.activation(out=nm12[h][:], in_=mx2[h][:], func=ACT.Copy, scale=-1.0)

        def exp12(h, i):
            junk = work.tile([P, 384], BF16, name="junk", bufs=2)
            A.activation(
                out=junk[:], in_=sc[h][:, i, 0:384], func=ACT.Exp, bias=nm12[h][:, i : i + 1], accum_out=s12[h][:, i : i + 1]
            )

        mx3, nm3, d3, s3, ln3, bias3 = {}, {}, {}, {}, {}, {}

        def last_max(h, x, bank):
            if h not in mx3:
                mx3[h] = keep.tile([P, 8], F32, name="mx3%d" % h)
            V.tensor_reduce(out=mx3[h][:, 4 * x : 4 * x + 4], in_=bank[:], axis=AX.X, op=ALU.max)
            A.activation(out=sc[h][:, 4 * x : 4 * x + 4, 384:512], in_=bank[:], func=ACT.Copy, scale=ALPHA)

        def last_shift(h):
            nm3[h] = keep.tile([P, 8], F32, name="nmf%d" % h)
            d3[h] = keep.tile([P, 8], F32, name="dd%d" % h)
            V.scalar_tensor_tensor(out=nm3[h][:], in0=mx3[h][:], scalar=-ALPHA, in1=nm12[h][:], op0=ALU.mult, op1=ALU.min)
            V.tensor_tensor(out=d3[h][:], in0=nm3[h][:], in1=nm12[h][:], op=ALU.subtract)

        def last_exps(h):
            s3[h] = keep.tile([P, 9, 8], F32, name="s3%d" % h)
            for i in range(8):
                junk = work.tile([P, 384], BF16, name="junk", bufs=2)
                A.activation(
                    out=junk[:, 0:128],
                    in_=sc[h][:, i, 384:512],
                    func=ACT.Exp,
                    bias=nm3[h][:, i : i + 1],
                    accum_out=s3[h][:, 0, i : i + 1],
                )
            A.activation(out=s3[h][:, 1, :], in_=d3[h][:], func=ACT.Exp)

        tot = {}

        def last_total(h):
            tot[h] = keep.tile([P, 8], F32, name="tot%d" % h)
            V.tensor_tensor(out=tot[h][:], in0=s12[h][:], in1=s3[h][:, 1, :], op=ALU.mult)
            V.tensor_tensor(out=tot[h][:], in0=tot[h][:], in1=s3[h][:, 0, :], op=ALU.add)

        def last_log(h):
            ln3[h] = keep.tile([P, 8], F32, name="ln%d" % h)
            A.activation(out=ln3[h][:], in_=tot[h][:], func=ACT.Ln, scale=1.0 / C)

        def last_bias(h):
            bias3[h] = keep.tile([P, 8], F32, name="bias%d" % h)
            V.tensor_tensor(out=bias3[h][:], in0=nm3[h][:], in1=ln3[h][:], op=ALU.subtract)

        def last_out(h, engines):
            dst = out[h].rearrange("(p i) c -> p i c", i=8)
            for i in range(8):
                row = sc[h][:, i, :]
                b = bias3[h][:, i : i + 1]
                if engines[i] == "a":
                    A.activation(out=row, in_=row, func=ACT.Identity, bias=b)
                elif engines[i] == "g":
                    G.tensor_scalar(out=row, in0=row, scalar1=1.0, scalar2=b, op0=ALU.mult, op1=ALU.add)
                else:
                    V.tensor_scalar(out=row, in0=row, scalar1=b, scalar2=None, op0=ALU.add)
                if i % 2 == 1:
                    SY.dma_start(out=dst[:, i - 1 : i + 1, :], in_=sc[h][:, i - 1 : i + 1, :])

        absolute(0, 0)
        table_cos(0, 0, 2)
        table_sin(0, 0, 2)
        widen(0, 0, range(8), range(8))
        xt = a_transpose(0, 0, "k0")
        widen(0, 1, range(8), (0, 1, 2, 3, 4, 5))
        a_evac(0, 0, xt, "v")
        xt = a_transpose(0, 1, "k0")
        a_quant(0, 0)
        mx(0)
        a_evac(0, 1, xt, "a")
        table_cos(0, 2, 2)
        table_sin(0, 2, 2)
        widen(0, 2, range(8), (0, 1, 2, 3, 4, 5))
        new_prod(0)
        products_v(0, 0)
        a_quant(0, 1)
        xt = a_transpose(0, 2)
        products_v(0, 1)
        widen(0, 3, range(8), (0, 1, 2, 3, 4, 5))
        a_evac(0, 2, xt, "a")
        absolute(0, 1)

        q_beats = {}
        for x in range(4):
            q_beats[6 + x] = (0, x)
            q_beats[14 + x] = (1, x)
        score_beats = {}
        for x in range(4):
            score_beats[15 + x] = (0, (2 * x, 2 * x + 1), 0, 256, mx1[0])
            score_beats[19 + x] = (1, (2 * x, 2 * x + 1), 0, 256, mx1[1])
        for x in range(2):
            score_beats[23 + x] = (0, tuple(range(4 * x, 4 * x + 4)), 256, 128, mx2[0])
            score_beats[27 + x] = (1, tuple(range(4 * x, 4 * x + 4)), 256, 128, mx2[1])

        SOFT0 = [[], [0], [1], [2], [3], [4], [5, 6], [7]]

        def soft(g, r):
            if r == 0:
                widen(g, 0, range(8), ())
                table_odd(g, 1)
            if r == 1:
                widen(g, 1, range(4), ())
            if r == 2:
                widen(g, 1, range(4, 8), ())
                widen(g, 2, range(8), ())
            if r == 3:
                widen(g, 3, range(8), ())
            if r == 4:
                table_cos(g, 0, 2)
                table_sin(g, 0, 1)
                table_cos(g, 2, 2)
            if r == 5:
                table_sin(g, 2, 2)
            if r == 6:
                table_odd(g, 5)
                table_cos(g, 4, 2)
                table_sin(g, 4, 1)
            if r == 7:
                table_cos(g, 6, 2)
                table_sin(g, 6, 2)

        for b in range(31):
            g, r, u, k = b // 8, b % 8, b // 4, b % 4
            n = b + 1
            if r == 0 and g + 1 < NG:
                for ap in range(4):
                    load_a(g + 1, ap)
                    if ap % 2 == 0:
                        load_theta(g + 1, ap // 2)
            if b in (1, 2):
                load_q(0, b - 1)
            if b in (9, 10):
                load_q(1, b - 9)
            mx(n)
            new_prod(n)
            if on_g(n):
                products_g(n)
            sbank = None
            if b in score_beats:
                h_s, tiles, c0, width, mxt = score_beats[b]
                sbank = scores(h_s, tiles, c0, width, "k0" if b < 22 else "misc")
            if b == 30:
                p3banks = [scores(0, tuple(range(4 * x, 4 * x + 4)), 384, 128, ("k0", "misc")[x]) for x in range(2)]
            if k == 1 and u > 0:
                lm_evac(u - 1, "aaaa")
                if u - 1 in MIX_A:
                    lm_mix(u - 1)
            if b == 0:
                a_quant(0, 2)
                xt = a_transpose(0, 3)
                a_evac(0, 3, xt, "a")
                table_cos(0, 4, 2)
                table_sin(0, 4, 1)
                table_odd(0, 5)
            if b == 1:
                a_quant(0, 3)
                table_cos(0, 6, 2)
                table_sin(0, 6, 2)
                table_s2(0, 1)
            if g + 1 < NG:
                if g == 0:
                    for x in SOFT0[r]:
                        soft(1, x)
                else:
                    soft(g + 1, r)
            if b == 25:
                max12(0)
            if b == 29:
                max12(1)
            if b in (25, 26, 29, 30):
                for x in range(3 if b == 30 else 4):
                    exp12(b // 29, 4 * ((b - 1) % 4 % 2) + x)
            if r == 1 and g + 1 < NG:
                absolute(g + 1, 0)
                absolute(g + 1, 1)
            if g + 1 < NG and r == 5:
                a_quant(g + 1, 0)
                if g > 0:
                    a_quant(g + 1, 1)
            if g + 1 < NG and r == 7:
                if g == 0:
                    a_quant(g + 1, 1)
                a_quant(g + 1, 2)
                a_quant(g + 1, 3)
            if b in (9, 11, 17, 19):
                for x in range(2):
                    q_quant(b // 17, 2 * ((b % 4) // 2) + x)
            products_v(n, 0)
            if sbank is not None and b < 22:
                scores_evac(h_s, tiles, c0, width, sbank, mxt)
            if b == 29:
                lm_quant(6)
            if not on_g(n):
                products_v(n, 1)
            if sbank is not None and b >= 22:
                scores_evac(h_s, tiles, c0, width, sbank, mxt)
            if b == 30:
                last_max(0, 0, p3banks[0])
                last_max(0, 1, p3banks[1])
                last_shift(0)
                last_exps(0)
            if k == 2 and 0 < u < 7:
                if u - 1 not in MIX_A:
                    lm_mix(u - 1)
                lm_quant(u - 1)
            ap = r - (3 if g == 0 else 2)
            if g + 1 < NG and 0 <= ap < 4:
                xt = a_transpose(g + 1, ap)
                a_evac(g + 1, ap, xt, "a")
            if b in q_beats:
                xt = q_transpose(*q_beats[b])
                q_evac(*q_beats[b], xt)
            if b >= 1:
                turn_and_add(b - 1, (b - 1) % 4 == 0, (b - 1) % 4 == 3)
        turn_and_add(30, False, False)
        turn_and_add(31, False, True)
        lm_evac(7, "vvvv")
        lm_mix(7)
        lm_quant(7)
        last_total(0)
        last_log(0)
        exp12(1, 7)
        last_bias(0)
        last_out(0, "vavvavva")
        for x in range(2):
            last_max(1, x, scores(1, tuple(range(4 * x, 4 * x + 4)), 384, 128, ("k0", "misc")[x]))
        last_shift(1)
        last_exps(1)
        last_total(1)
        last_log(1)
        last_bias(1)
        last_out(1, "vavvavva")
